import numpy as np
import ml_dtypes


def mxq(x, axis, fmt="e4m3"):
    dtype, down = {"e4m3": (ml_dtypes.float8_e4m3fn, 7), "e5m2": (ml_dtypes.float8_e5m2, 14)}[fmt]
    v = np.moveaxis(np.asarray(x, np.float32).astype(ml_dtypes.bfloat16).astype(np.float64), axis, -1)
    blocks = v.reshape(v.shape[:-1] + (-1, 32))
    amax = np.abs(blocks).max(-1, keepdims=True)
    byte = np.maximum(np.where(amax > 0, np.frexp(amax)[1] - 1 + 127, 0) - down, 1)
    scale = np.exp2(byte - 127.0)
    codes = (blocks / scale).astype(np.float32).astype(dtype).astype(np.float64)
    return np.moveaxis((codes * scale).reshape(v.shape), -1, axis)


WIDE = False


def mx_kscale(k):
    if not WIDE:
        return np.ones(k)
    levels = np.array([10, -10, 5, -5, 0])
    if k % 512:
        return np.exp2(np.random.permutation(np.resize(levels, k // 32))).repeat(32)
    a = np.empty((k // 512, 16))
    for p in range(k // 512):
        a[p, :8] = np.random.permutation(np.resize(levels, 8))
        for g in range(8):
            far = levels[np.abs(levels - a[p, g]) >= 10]
            a[p, g + 8] = far[np.random.randint(len(far))]
    return np.exp2(a.ravel()).repeat(32)


def f64(x):
    return np.asarray(x).astype(np.float64)


def striped(idx):
    return np.tile(idx.reshape(-1, 16).T, (8, 1)).astype(np.uint16)


def unstriped(offs):
    return offs[:16].T.reshape(-1).astype(np.int64)


E2M1 = np.array([0.0, 0.5, 1.0, 1.5, 2.0, 3.0, 4.0, 6.0, -0.0, -0.5, -1.0, -1.5, -2.0, -3.0, -4.0, -6.0])


def pack_weight(w, fmt):
    k, n = w.shape
    w = f64(np.asarray(w, np.float32).astype(ml_dtypes.bfloat16)).reshape(k // 32, 32, n)
    amax = np.abs(w).max(1)
    if fmt == "e4m3":
        byte = np.frexp(amax)[1] - 1 + 127 - 7
    else:
        mant, ex = np.frexp(amax / 6.0)
        byte = np.where(mant > 0.5, ex, ex - 1) + 127
    byte = np.clip(np.where(amax > 0, byte, 1), 1, 254)
    scaled = (w * np.exp2(127.0 - byte)[:, None, :]).reshape(k, n).astype(np.float32)
    by_word = np.ascontiguousarray(scaled.reshape(k // 512, 128, 4, n).transpose(0, 1, 3, 2))
    if fmt == "e4m3":
        words = by_word.astype(ml_dtypes.float8_e4m3fn).view(np.uint8)
    else:
        c = by_word.astype(ml_dtypes.float4_e2m1fn).view(np.uint8) & 0xF
        words = (c[..., 0::2] | (c[..., 1::2] << 4)).reshape(k // 512, 128, 2 * n)
    return np.ascontiguousarray(words), np.ascontiguousarray(byte.astype(np.uint8).reshape(k // 512, 16, n))


def unpack_weight(words, scales, fmt):
    g, _, n = scales.shape
    words = np.ascontiguousarray(words).reshape(g, 128, n, -1)
    if fmt == "e4m3":
        vals = words.view(ml_dtypes.float8_e4m3fn).astype(np.float64)
    else:
        nib = np.empty((g, 128, n, 4), np.uint8)
        nib[..., 0::2] = words & 0xF
        nib[..., 1::2] = words >> 4
        vals = E2M1[nib]
    vals = vals * np.repeat(np.exp2(scales.astype(np.float64) - 127.0), 8, axis=1)[..., None]
    return vals.transpose(0, 1, 3, 2).reshape(g * 512, n)


def planes(y):
    n, m = y.shape
    v = y.astype(np.float32).astype(ml_dtypes.bfloat16).astype(np.float64).reshape(n // 32, 32, m)
    top = np.abs(v).max(1)
    byte = np.clip(np.where(top > 0, np.frexp(top)[1] - 1 + 127 - 7, 1), 1, 254)
    codes = (v * np.exp2(127.0 - byte)[:, None, :]).reshape(n, m).astype(np.float32).astype(ml_dtypes.float8_e4m3fn).view(np.uint8)
    words = codes.reshape(n // 512, 128, 4, m).transpose(0, 1, 3, 2)
    return np.ascontiguousarray(words), np.ascontiguousarray(byte.astype(np.uint8).reshape(n // 512, 16, m))


def d_relu2(v):
    return 2.0 * np.maximum(v, 0.0)


K, T, E, C, H, N = 512, 512, 4, 128, 512, 512


def by_expert(wq, xq):
    return np.concatenate([wq[e].T @ xq[:, e * C:(e + 1) * C] for e in range(E)], axis=1)


def setup_inputs():
    n = np.random.standard_normal
    s = mx_kscale(K)
    v = mx_kscale(N)
    u = mx_kscale(H)
    slot_token = np.random.permutation(T)[:E * C]
    w_slot = np.random.uniform(0.2, 1.0, E * C)
    x = pack_weight(n((K, T)) * s[:, None], "e4m3")
    dy = pack_weight(n((N, T)) * v[:, None], "e4m3")
    m1 = n((E, K, H))
    w1 = [pack_weight(m, "e4m3") for m in m1 / np.sqrt(K) / s[None, :, None]]
    w2t = [pack_weight(m, "e4m3") for m in n((E, N, H)) / np.sqrt(N) / v[None, :, None] * u]
    w1t = [pack_weight(m, "e4m3") for m in m1.transpose(0, 2, 1) / np.sqrt(H) / u[None, :, None]]
    return {
        "x_words": x[0],
        "x_scales": x[1],
        "dy_words": dy[0],
        "dy_scales": dy[1],
        "w1_words": np.stack([m[0] for m in w1]),
        "w1_scales": np.stack([m[1] for m in w1]),
        "w2t_words": np.stack([m[0] for m in w2t]),
        "w2t_scales": np.stack([m[1] for m in w2t]),
        "w1t_words": np.stack([m[0] for m in w1t]),
        "w1t_scales": np.stack([m[1] for m in w1t]),
        "gate": (np.tile(w_slot, (128, 1))).astype(np.float32),
        "offs": striped(slot_token),
    }


def reference(x_words, x_scales, dy_words, dy_scales, w1_words, w1_scales, w2t_words, w2t_scales, w1t_words, w1t_scales, gate, offs):
    w1 = np.stack([unpack_weight(w1_words[e], w1_scales[e], "e4m3") for e in range(E)])
    w2t = np.stack([unpack_weight(w2t_words[e], w2t_scales[e], "e4m3") for e in range(E)])
    w1t = np.stack([unpack_weight(w1t_words[e], w1t_scales[e], "e4m3") for e in range(E)])
    idx = unstriped(offs)
    xq = unpack_weight(x_words, x_scales, "e4m3")[:, idx]
    gq = unpack_weight(dy_words, dy_scales, "e4m3")[:, idx]
    dh = f64(gate[:1]) * by_expert(w2t, gq)
    a = by_expert(w1, xq)
    dx = by_expert(w1t, mxq(dh * d_relu2(a), 0, "e4m3"))
    out = np.zeros((K, T))
    out[:, idx] = dx
    out_0 = out
    return (out_0,) + planes(out_0)

@@ -1,0 +1,219 @@
+from contextlib import ExitStack
+
+import concourse.mybir as mybir
+from concourse.masks import make_identity
+
+K, T, E, C, H, N = 512, 512, 4, 128, 512, 512
+FLOPS = 3 * 2 * 512 * 512 * 512
+
+F32 = mybir.dt.float32
+BF16 = mybir.dt.bfloat16
+I32 = mybir.dt.int32
+U32 = mybir.dt.uint32
+U16 = mybir.dt.uint16
+U8 = mybir.dt.uint8
+FP8X4 = mybir.dt.float8_e4m3fn_x4
+MULT = mybir.AluOpType.mult
+RELU = mybir.ActivationFunctionType.Relu
+COPY = mybir.ActivationFunctionType.Copy
+
+P = 128
+PACK = 4
+QUADS = 4
+LIST_COLS = C // 16
+HALF = T // 2
+
+
+def tile_moe_rec_mlp_relu2_kernel(
+    tc, x_words, x_scales, dy_words, dy_scales, w1_words, w1_scales, w2t_words, w2t_scales,
+    w1t_words, w1t_scales, gate, offs, out_0, out_1, out_2,
+):
+    nc = tc.nc
+    with ExitStack() as ctx:
+        sb = ctx.enter_context(tc.tile_pool(name="sb", bufs=1))
+        ps = ctx.enter_context(tc.psum_pool(name="ps", bufs=1))
+
+        def tile(name, shape, dtype, over=None):
+            return sb.tile(shape, dtype, name=name, tag=over or name, align_bytes=64)
+
+        def bank_tile(name, shape, bank):
+            return ps.tile(shape, F32, name=name, tag=f"bank{bank}")
+
+        offsets = sb.tile([P, E * LIST_COLS], U16, name="offsets")
+        x_w, dy_w = tile("x_w", [P, T], U32), tile("dy_w", [P, T], U32)
+        x_s, dy_s = tile("x_s", [P, T], U8), tile("dy_s", [P, T], U8)
+        w1_s, w2t_s, w1t_s = tile("w1_s", [P, H], U8), tile("w2t_s", [P, H], U8), tile("w1t_s", [P, K], U8)
+        gate_rows = tile("gate_rows", [P, C], F32)
+        ident = tile("ident", [P, P], F32)
+
+        for plane in (x_s, w1_s, dy_s):
+            nc.vector.memset(plane[:].bitcast(I32), 0)
+        for plane in (w2t_s, w1t_s):
+            nc.gpsimd.memset(plane[:].bitcast(I32), 0)
+        nc.gpsimd.memset(gate_rows[:], 0.0)
+        make_identity(nc, ident[:])
+
+        def load_token_words(dst, words):
+            nc.sync.dma_start(dst[:].bitcast(I32), words[0].rearrange("p n d -> p (n d)").bitcast(I32))
+
+        def load_token_scales(dst, scales, quads):
+            for q in quads:
+                nc.sync.dma_start(dst[32 * q : 32 * q + 4, :].bitcast(I32), scales[0, 4 * q : 4 * q + 4, :].bitcast(I32))
+
+        def load_weight_scales(dst, scales):
+            for q in range(QUADS):
+                nc.sync.dma_start(
+                    dst[32 * q : 32 * q + 4 * E, :].bitcast(I32), scales[:, 0, 4 * q : 4 * q + 4, :].bitcast(I32)
+                )
+
+        w = {}
+
+        def load_weight(name, words, e0, e1):
+            dst = tile(f"{name}_{e0}", [P, e1 - e0, 512], U32)
+            nc.sync.dma_start(dst[:].bitcast(I32), words[e0:e1, 0].rearrange("e p n d -> p e (n d)").bitcast(I32))
+            for e in range(e0, e1):
+                w[name, e] = dst[:, e - e0, :]
+
+        nc.sync.dma_start(offsets[:], offs)
+        load_token_words(x_w, x_words)
+        load_token_scales(x_s, x_scales, range(QUADS))
+        load_token_words(dy_w, dy_words)
+        load_weight("w1", w1_words, 0, 2)
+        load_weight_scales(w1_s, w1_scales)
+        load_token_scales(dy_s, dy_scales, range(QUADS - 1))
+        load_weight("w2t", w2t_words, 0, 2)
+        load_token_scales(dy_s, dy_scales, range(QUADS - 1, QUADS))
+        load_weight_scales(w2t_s, w2t_scales)
+        nc.sync.dma_start(gate_rows[0:E, :], gate[0].rearrange("(e u) -> e u", e=E))
+        load_weight("w1t", w1t_words, 0, 1)
+        load_weight("w1", w1_words, 2, 4)
+        load_weight_scales(w1t_s, w1t_scales)
+        load_weight("w2t", w2t_words, 2, 4)
+        load_weight("w1t", w1t_words, 1, 2)
+        load_weight("w1t", w1t_words, 2, 4)
+
+        def slots(e):
+            return offsets[:, e * LIST_COLS : (e + 1) * LIST_COLS]
+
+        gathered = {}
+
+        def gather(name, words, scales, e0):
+            g_w, g_s = tile(f"{name}_gw{e0}", [P, 2 * C], U32), tile(f"{name}_gs{e0}", [P, 2 * C], U8)
+            pair = offsets[:, e0 * LIST_COLS : (e0 + 2) * LIST_COLS]
+            nc.vector.tensor_copy(g_w[:], words[:].indirect(pair))
+            nc.vector.tensor_copy(g_s[:], scales[:].indirect(pair))
+            for j in range(2):
+                gathered[name, e0 + j] = (g_w[:, j * C : (j + 1) * C], g_s[:, j * C : (j + 1) * C])
+
+        for e0 in (0, 2):
+            gather("x", x_w, x_s, e0)
+            gather("dy", dy_w, dy_s, e0)
+
+        def first_product(name, first_bank, tokens, plane, e):
+            bank = bank_tile(f"{name}_sum{e}", [P, H], first_bank + e % 2)
+            nc.tensor.matmul_mx(
+                bank[:], lhsT=tokens[0].bitcast(FP8X4), lhsT_scale=tokens[1],
+                rhs=w[name, e].bitcast(FP8X4), rhs_scale=plane[4 * e : P, :], start=True, stop=True,
+            )
+            return bank
+
+        slope = {}
+        for e in range(E):
+            a = first_product("w1", 0, gathered["x", e], w1_s, e)
+            slope[e] = tile(f"slope{e}", [P, H], F32)
+            nc.scalar.activation(slope[e][:], a[:], RELU, scale=2.0)
+
+        gate_turned = bank_tile("gate_turned", [P, 2, P], 5)
+        nc.tensor.transpose(gate_turned[:, 0, :], gate_rows[:], ident[:])
+        gate_cols = tile("gate_cols", [P, E], F32)
+        nc.scalar.copy(gate_cols[:], gate_turned[:, 0, 0:E])
+
+        w1t_s_dealt = tile("w1t_s_dealt", [P, K], U8)
+        nc.vector.tensor_copy(
+            w1t_s_dealt[:].rearrange("p (t m) -> p t m", t=PACK), w1t_s[:].rearrange("p (m t) -> p t m", t=PACK)
+        )
+
+        def deal(e):
+            dealt = tile(f"w1t_dealt{e}", [P, K], U32)
+            dst = dealt[:].rearrange("p (t c i) -> p c t i", t=PACK, i=4)
+            src = w["w1t", e].rearrange("p (c i t) -> p c t i", t=PACK, i=4)
+            if e < 2:
+                nc.scalar.copy(dst, src)
+            else:
+                nc.vector.tensor_copy(
+                    dealt[:].bitcast(I32).rearrange("p (t c i) -> p c t i", t=PACK, i=4),
+                    w["w1t", e].bitcast(I32).rearrange("p (c i t) -> p c t i", t=PACK, i=4),
+                )
+            return dealt
+
+        da_mx, dx = {}, {}
+
+        def hidden(e):
+            dh = first_product("w2t", 2, gathered["dy", e], w2t_s, e)
+            da = tile(f"da{e}", [P, H], BF16)
+            nc.vector.scalar_tensor_tensor(da[:], dh[:], gate_cols[:, e : e + 1], slope[e][:], MULT, MULT)
+            pairs = da[:].bitcast(F32)
+            turned = bank_tile(f"turned{e}", [P, 2, P], 4 + e % 2)
+            for u in range(2):
+                nc.tensor.transpose(turned[:, u, :], pairs[:, u : H // 2 : 2], ident[:])
+            grouped = tile(f"da_grouped{e}", [P, C * PACK], BF16)
+            nc.scalar.copy(grouped[:].bitcast(F32).rearrange("p (j u) -> p j u", u=2), turned[:].rearrange("p u j -> p j u"))
+            codes, scales = tile(f"da_w{e}", [P, C], U32), tile(f"da_s{e}", [P, C], U8)
+            nc.vector.quantize_mx(codes[:].bitcast(FP8X4), scales[:], grouped[:])
+            da_mx[e] = (codes, scales)
+
+        def second_product(e):
+            dealt = deal(e)
+            codes, scales = da_mx[e]
+            bank = bank_tile(f"dx_sum{e}", [P, PACK, C], (6, 7, 0, 1)[e])
+            for t in range(PACK):
+                cols = slice(t * P, (t + 1) * P)
+                nc.tensor.matmul_mx(
+                    bank[:, t, :], lhsT=dealt[:, cols].bitcast(FP8X4), lhsT_scale=w1t_s_dealt[4 * e : P, cols],
+                    rhs=codes[:].bitcast(FP8X4), rhs_scale=scales[:], start=True, stop=True,
+                )
+            dx[e] = tile(f"dx{e}", [P, PACK, C], F32)
+            nc.scalar.copy(dx[e][:], bank[:])
+
+        def scatter(e):
+            for t in range(2):
+                nc.vector.tensor_copy(windows[t][:].indirect(slots(e)), dx[e][:, t, :])
+                nc.scalar.activation(windows[t + 2][:].indirect(slots(e)), dx[e][:, t + 2, :], COPY)
+
+        hidden(0)
+        hidden(1)
+        second_product(0)
+        hidden(2)
+        second_product(1)
+        hidden(3)
+        second_product(2)
+        second_product(3)
+        over = ("slope3", "da_grouped2", "da3", "da2")
+        windows = [tile(f"window{t}", [P, T], F32, over[t]) for t in range(PACK)]
+        for e in range(E):
+            scatter(e)
+
+        rows = out_0.rearrange("(p t) n -> t p n", t=PACK)
+        rounded = tile("rounded", [P, PACK, T], BF16)
+        for t in (0, 2, 1, 3):
+            nc.sync.dma_start(rows[t], windows[t][:])
+            if t < 3:
+                nc.vector.tensor_copy(rounded[:, t, :], windows[t][:])
+            else:
+                nc.scalar.copy(rounded[:, t, :], windows[t][:])
+
+        out_w, out_s = tile("out_w", [P, T], U32), tile("out_s", [P, T], U8)
+        out_words = out_1[0].rearrange("p n d -> p (n d)").bitcast(I32)
+        for h in range(2):
+            cols = slice(h * HALF, (h + 1) * HALF)
+            woven = tile(f"woven{h}", [P, HALF * PACK], BF16)
+            dst = woven[:].rearrange("p (c i t) -> p c t i", t=PACK, i=4)
+            src = rounded[:, :, cols].rearrange("p t (c i) -> p c t i", i=4)
+            if h == 0:
+                nc.vector.tensor_copy(dst, src)
+            else:
+                nc.scalar.copy(dst, src)
+            nc.vector.quantize_mx(out_w[:, cols].bitcast(FP8X4), out_s[:, cols], woven[:])
+            nc.sync.dma_start(out_words[:, cols], out_w[:, cols].bitcast(I32))
+        for q in range(QUADS):
+            nc.sync.dma_start(out_2[0, 4 * q : 4 * q + 4, :].bitcast(I32), out_s[32 * q : 32 * q + 4, :].bitcast(I32))

@@ -46,12 +46,11 @@ def tile_moe_rec_mlp_relu2_kernel(
         gate_rows = tile("gate_rows", [P, C], F32)
         ident = tile("ident", [P, P], F32)
 
-        for plane in (x_s, w1_s, dy_s):
+        nc.vector.memset(ident[:], 0.0)
+        for plane in (w1t_s, x_s, w1_s, dy_s, w2t_s):
             nc.vector.memset(plane[:].bitcast(I32), 0)
-        for plane in (w2t_s, w1t_s):
-            nc.gpsimd.memset(plane[:].bitcast(I32), 0)
-        nc.gpsimd.memset(gate_rows[:], 0.0)
-        make_identity(nc, ident[:])
+        nc.vector.memset(gate_rows[:], 0.0)
+        make_identity(nc, ident[:], nomemset=True)
 
         def load_token_words(dst, words):
             nc.sync.dma_start(dst[:].bitcast(I32), words[0].rearrange("p n d -> p (n d)").bitcast(I32))
@@ -60,9 +59,9 @@ def tile_moe_rec_mlp_relu2_kernel(
             for q in quads:
                 nc.sync.dma_start(dst[32 * q : 32 * q + 4, :].bitcast(I32), scales[0, 4 * q : 4 * q + 4, :].bitcast(I32))
 
-        def load_weight_scales(dst, scales):
+        def load_weight_scales(dst, scales, queue=nc.sync):
             for q in range(QUADS):
-                nc.sync.dma_start(
+                queue.dma_start(
                     dst[32 * q : 32 * q + 4 * E, :].bitcast(I32), scales[:, 0, 4 * q : 4 * q + 4, :].bitcast(I32)
                 )
 
@@ -80,17 +79,15 @@ def tile_moe_rec_mlp_relu2_kernel(
         load_token_words(dy_w, dy_words)
         load_weight("w1", w1_words, 0, 2)
         load_weight_scales(w1_s, w1_scales)
-        load_token_scales(dy_s, dy_scales, range(QUADS - 1))
-        load_weight("w2t", w2t_words, 0, 2)
-        load_token_scales(dy_s, dy_scales, range(QUADS - 1, QUADS))
-        load_weight_scales(w2t_s, w2t_scales)
-        nc.sync.dma_start(gate_rows[0:E, :], gate[0].rearrange("(e u) -> e u", e=E))
-        load_weight("w1t", w1t_words, 0, 1)
         load_weight("w1", w1_words, 2, 4)
-        load_weight_scales(w1t_s, w1t_scales)
+        load_token_scales(dy_s, dy_scales, range(QUADS))
+        load_weight("w2t", w2t_words, 0, 2)
+        nc.sync.dma_start(gate_rows[0:E, :], gate[0].rearrange("(e u) -> e u", e=E))
+        load_weight_scales(w2t_s, w2t_scales)
         load_weight("w2t", w2t_words, 2, 4)
-        load_weight("w1t", w1t_words, 1, 2)
+        load_weight("w1t", w1t_words, 0, 2)
         load_weight("w1t", w1t_words, 2, 4)
+        load_weight_scales(w1t_s, w1t_scales, nc.gpsimd)
 
         def slots(e):
             return offsets[:, e * LIST_COLS : (e + 1) * LIST_COLS]
@@ -110,7 +107,7 @@ def tile_moe_rec_mlp_relu2_kernel(
             gather("dy", dy_w, dy_s, e0)
 
         def first_product(name, first_bank, tokens, plane, e):
-            bank = bank_tile(f"{name}_sum{e}", [P, H], first_bank + e % 2)
+            bank = bank_tile(f"{name}_sum{e}", [P, H], first_bank + e)
             nc.tensor.matmul_mx(
                 bank[:], lhsT=tokens[0].bitcast(FP8X4), lhsT_scale=tokens[1],
                 rhs=w[name, e].bitcast(FP8X4), rhs_scale=plane[4 * e : P, :], start=True, stop=True,
@@ -123,12 +120,12 @@ def tile_moe_rec_mlp_relu2_kernel(
             slope[e] = tile(f"slope{e}", [P, H], F32)
             nc.scalar.activation(slope[e][:], a[:], RELU, scale=2.0)
 
-        gate_turned = bank_tile("gate_turned", [P, 2, P], 5)
+        gate_turned = bank_tile("gate_turned", [P, 2, P], 4)
         nc.tensor.transpose(gate_turned[:, 0, :], gate_rows[:], ident[:])
         gate_cols = tile("gate_cols", [P, E], F32)
         nc.scalar.copy(gate_cols[:], gate_turned[:, 0, 0:E])
 
-        w1t_s_dealt = tile("w1t_s_dealt", [P, K], U8)
+        w1t_s_dealt = tile("w1t_s_dealt", [P, K], U8, "dy_s")
         nc.vector.tensor_copy(
             w1t_s_dealt[:].rearrange("p (t m) -> p t m", t=PACK), w1t_s[:].rearrange("p (m t) -> p t m", t=PACK)
         )
@@ -137,7 +134,7 @@ def tile_moe_rec_mlp_relu2_kernel(
             dealt = tile(f"w1t_dealt{e}", [P, K], U32)
             dst = dealt[:].rearrange("p (t c i) -> p c t i", t=PACK, i=4)
             src = w["w1t", e].rearrange("p (c i t) -> p c t i", t=PACK, i=4)
-            if e < 2:
+            if "VSVV"[e] == "S":
                 nc.scalar.copy(dst, src)
             else:
                 nc.vector.tensor_copy(
@@ -149,11 +146,11 @@ def tile_moe_rec_mlp_relu2_kernel(
         da_mx, dx = {}, {}
 
         def hidden(e):
-            dh = first_product("w2t", 2, gathered["dy", e], w2t_s, e)
+            dh = first_product("w2t", 4, gathered["dy", e], w2t_s, e)
             da = tile(f"da{e}", [P, H], BF16)
             nc.vector.scalar_tensor_tensor(da[:], dh[:], gate_cols[:, e : e + 1], slope[e][:], MULT, MULT)
             pairs = da[:].bitcast(F32)
-            turned = bank_tile(f"turned{e}", [P, 2, P], 4 + e % 2)
+            turned = bank_tile(f"turned{e}", [P, 2, P], e % 2)
             for u in range(2):
                 nc.tensor.transpose(turned[:, u, :], pairs[:, u : H // 2 : 2], ident[:])
             grouped = tile(f"da_grouped{e}", [P, C * PACK], BF16)
@@ -165,7 +162,7 @@ def tile_moe_rec_mlp_relu2_kernel(
         def second_product(e):
             dealt = deal(e)
             codes, scales = da_mx[e]
-            bank = bank_tile(f"dx_sum{e}", [P, PACK, C], (6, 7, 0, 1)[e])
+            bank = bank_tile(f"dx_sum{e}", [P, PACK, C], 2 + e)
             for t in range(PACK):
                 cols = slice(t * P, (t + 1) * P)
                 nc.tensor.matmul_mx(
@@ -173,12 +170,17 @@ def tile_moe_rec_mlp_relu2_kernel(
                     rhs=codes[:].bitcast(FP8X4), rhs_scale=scales[:], start=True, stop=True,
                 )
             dx[e] = tile(f"dx{e}", [P, PACK, C], F32)
-            nc.scalar.copy(dx[e][:], bank[:])
+            if "VSSS"[e] == "S":
+                nc.scalar.copy(dx[e][:], bank[:])
+            else:
+                nc.vector.tensor_copy(dx[e][:], bank[:])
 
         def scatter(e):
-            for t in range(2):
-                nc.vector.tensor_copy(windows[t][:].indirect(slots(e)), dx[e][:, t, :])
-                nc.scalar.activation(windows[t + 2][:].indirect(slots(e)), dx[e][:, t + 2, :], COPY)
+            for t in (0, 2, 1, 3):
+                if ["VVSS","VVSS","VVSS","VVSS"][e][t] == "V":
+                    nc.vector.tensor_copy(windows[t][:].indirect(slots(e)), dx[e][:, t, :])
+                else:
+                    nc.scalar.activation(windows[t][:].indirect(slots(e)), dx[e][:, t, :], COPY)
 
         hidden(0)
         hidden(1)
@@ -188,7 +190,7 @@ def tile_moe_rec_mlp_relu2_kernel(
         hidden(3)
         second_product(2)
         second_product(3)
-        over = ("slope3", "da_grouped2", "da3", "da2")
+        over = (None, None, None, None)
         windows = [tile(f"window{t}", [P, T], F32, over[t]) for t in range(PACK)]
         for e in range(E):
             scatter(e)
@@ -197,7 +199,7 @@ def tile_moe_rec_mlp_relu2_kernel(
         rounded = tile("rounded", [P, PACK, T], BF16)
         for t in (0, 2, 1, 3):
             nc.sync.dma_start(rows[t], windows[t][:])
-            if t < 3:
+            if "VVSV"[t] == "V":
                 nc.vector.tensor_copy(rounded[:, t, :], windows[t][:])
             else:
                 nc.scalar.copy(rounded[:, t, :], windows[t][:])
@@ -216,4 +218,4 @@ def tile_moe_rec_mlp_relu2_kernel(
             nc.vector.quantize_mx(out_w[:, cols].bitcast(FP8X4), out_s[:, cols], woven[:])
             nc.sync.dma_start(out_words[:, cols], out_w[:, cols].bitcast(I32))
         for q in range(QUADS):
-            nc.sync.dma_start(out_2[0, 4 * q : 4 * q + 4, :].bitcast(I32), out_s[32 * q : 32 * q + 4, :].bitcast(I32))
+            (nc.sync, nc.scalar)[q % 2].dma_start(out_2[0, 4 * q : 4 * q + 4, :].bitcast(I32), out_s[32 * q : 32 * q + 4, :].bitcast(I32))

@@ -4,7 +4,7 @@ import concourse.mybir as mybir
 from concourse.masks import make_identity
 
 K, T, E, C, H, N = 512, 512, 4, 128, 512, 512
-FLOPS = 3 * 2 * 512 * 512 * 512
+FLOPS = 2 * E * C * (K * H + N * H + H * K)
 
 F32 = mybir.dt.float32
 BF16 = mybir.dt.bfloat16
@@ -20,8 +20,18 @@ COPY = mybir.ActivationFunctionType.Copy
 P = 128
 PACK = 4
 QUADS = 4
+LINE = 4
 LIST_COLS = C // 16
+SCALE_ROWS = 4
+PAIR = 2
 HALF = T // 2
+
+VECTOR_WINDOWS = 2
+DEALT_ON_SCALAR = 1
+EMPTIED_ON_VECTOR = 0
+ROUNDED_ON_SCALAR = VECTOR_WINDOWS
+
+A_BANK, DH_BANK, DX_BANK = 0, E, 2
 
 
 def tile_moe_rec_mlp_relu2_kernel(
@@ -39,6 +49,12 @@ def tile_moe_rec_mlp_relu2_kernel(
         def bank_tile(name, shape, bank):
             return ps.tile(shape, F32, name=name, tag=f"bank{bank}")
 
+        def copy_on(on_vector, dst, src):
+            if on_vector:
+                nc.vector.tensor_copy(dst, src)
+            else:
+                nc.scalar.copy(dst, src)
+
         offsets = sb.tile([P, E * LIST_COLS], U16, name="offsets")
         x_w, dy_w = tile("x_w", [P, T], U32), tile("dy_w", [P, T], U32)
         x_s, dy_s = tile("x_s", [P, T], U8), tile("dy_s", [P, T], U8)
@@ -55,54 +71,58 @@ def tile_moe_rec_mlp_relu2_kernel(
         def load_token_words(dst, words):
             nc.sync.dma_start(dst[:].bitcast(I32), words[0].rearrange("p n d -> p (n d)").bitcast(I32))
 
-        def load_token_scales(dst, scales, quads):
-            for q in quads:
-                nc.sync.dma_start(dst[32 * q : 32 * q + 4, :].bitcast(I32), scales[0, 4 * q : 4 * q + 4, :].bitcast(I32))
+        def scale_rows(q):
+            return slice(SCALE_ROWS * q, SCALE_ROWS * (q + 1))
 
-        def load_weight_scales(dst, scales, queue=nc.sync):
+        def load_token_scales(dst, scales):
             for q in range(QUADS):
-                queue.dma_start(
-                    dst[32 * q : 32 * q + 4 * E, :].bitcast(I32), scales[:, 0, 4 * q : 4 * q + 4, :].bitcast(I32)
+                nc.sync.dma_start(
+                    dst[32 * q : 32 * q + SCALE_ROWS, :].bitcast(I32), scales[0, scale_rows(q), :].bitcast(I32)
                 )
 
-        w = {}
+        def load_weight_scales(queue, dst, scales):
+            for q in range(QUADS):
+                queue.dma_start(
+                    dst[32 * q : 32 * q + SCALE_ROWS * E, :].bitcast(I32), scales[:, 0, scale_rows(q), :].bitcast(I32)
+                )
 
-        def load_weight(name, words, e0, e1):
-            dst = tile(f"{name}_{e0}", [P, e1 - e0, 512], U32)
-            nc.sync.dma_start(dst[:].bitcast(I32), words[e0:e1, 0].rearrange("e p n d -> p e (n d)").bitcast(I32))
-            for e in range(e0, e1):
-                w[name, e] = dst[:, e - e0, :]
+        weight = {}
+
+        def load_weight(name, words, e0):
+            dst = tile(f"{name}_{e0}", [P, PAIR, 512], U32)
+            src = words[e0 : e0 + PAIR, 0].rearrange("e p n d -> p e (n d)")
+            nc.sync.dma_start(dst[:].bitcast(I32), src.bitcast(I32))
+            for j in range(PAIR):
+                weight[name, e0 + j] = dst[:, j, :]
+
+        def load_weight_and_scales(name, words, scales_queue, plane, scales):
+            load_weight(name, words, 0)
+            load_weight_scales(scales_queue, plane, scales)
+            load_weight(name, words, PAIR)
 
         nc.sync.dma_start(offsets[:], offs)
         load_token_words(x_w, x_words)
-        load_token_scales(x_s, x_scales, range(QUADS))
+        load_token_scales(x_s, x_scales)
         load_token_words(dy_w, dy_words)
-        load_weight("w1", w1_words, 0, 2)
-        load_weight_scales(w1_s, w1_scales)
-        load_weight("w1", w1_words, 2, 4)
-        load_token_scales(dy_s, dy_scales, range(QUADS))
-        load_weight("w2t", w2t_words, 0, 2)
+        load_weight_and_scales("w1", w1_words, nc.sync, w1_s, w1_scales)
+        load_token_scales(dy_s, dy_scales)
         nc.sync.dma_start(gate_rows[0:E, :], gate[0].rearrange("(e u) -> e u", e=E))
-        load_weight_scales(w2t_s, w2t_scales)
-        load_weight("w2t", w2t_words, 2, 4)
-        load_weight("w1t", w1t_words, 0, 2)
-        load_weight("w1t", w1t_words, 2, 4)
-        load_weight_scales(w1t_s, w1t_scales, nc.gpsimd)
+        load_weight_and_scales("w2t", w2t_words, nc.sync, w2t_s, w2t_scales)
+        load_weight_and_scales("w1t", w1t_words, nc.gpsimd, w1t_s, w1t_scales)
 
-        def slots(e):
-            return offsets[:, e * LIST_COLS : (e + 1) * LIST_COLS]
+        def entries(e0, e1):
+            return offsets[:, e0 * LIST_COLS : e1 * LIST_COLS]
 
         gathered = {}
 
         def gather(name, words, scales, e0):
-            g_w, g_s = tile(f"{name}_gw{e0}", [P, 2 * C], U32), tile(f"{name}_gs{e0}", [P, 2 * C], U8)
-            pair = offsets[:, e0 * LIST_COLS : (e0 + 2) * LIST_COLS]
-            nc.vector.tensor_copy(g_w[:], words[:].indirect(pair))
-            nc.vector.tensor_copy(g_s[:], scales[:].indirect(pair))
-            for j in range(2):
+            g_w, g_s = tile(f"{name}_gw{e0}", [P, PAIR * C], U32), tile(f"{name}_gs{e0}", [P, PAIR * C], U8)
+            nc.vector.tensor_copy(g_w[:], words[:].indirect(entries(e0, e0 + PAIR)))
+            nc.vector.tensor_copy(g_s[:], scales[:].indirect(entries(e0, e0 + PAIR)))
+            for j in range(PAIR):
                 gathered[name, e0 + j] = (g_w[:, j * C : (j + 1) * C], g_s[:, j * C : (j + 1) * C])
 
-        for e0 in (0, 2):
+        for e0 in range(0, E, PAIR):
             gather("x", x_w, x_s, e0)
             gather("dy", dy_w, dy_s, e0)
 
@@ -110,112 +130,101 @@ def tile_moe_rec_mlp_relu2_kernel(
             bank = bank_tile(f"{name}_sum{e}", [P, H], first_bank + e)
             nc.tensor.matmul_mx(
                 bank[:], lhsT=tokens[0].bitcast(FP8X4), lhsT_scale=tokens[1],
-                rhs=w[name, e].bitcast(FP8X4), rhs_scale=plane[4 * e : P, :], start=True, stop=True,
+                rhs=weight[name, e].bitcast(FP8X4), rhs_scale=plane[SCALE_ROWS * e : P, :], start=True, stop=True,
             )
             return bank
 
         slope = {}
         for e in range(E):
-            a = first_product("w1", 0, gathered["x", e], w1_s, e)
+            a = first_product("w1", A_BANK, gathered["x", e], w1_s, e)
             slope[e] = tile(f"slope{e}", [P, H], F32)
             nc.scalar.activation(slope[e][:], a[:], RELU, scale=2.0)
 
-        gate_turned = bank_tile("gate_turned", [P, 2, P], 4)
-        nc.tensor.transpose(gate_turned[:, 0, :], gate_rows[:], ident[:])
+        gate_turned = bank_tile("gate_turned", [P, P], DH_BANK)
+        nc.tensor.transpose(gate_turned[:], gate_rows[:], ident[:])
         gate_cols = tile("gate_cols", [P, E], F32)
-        nc.scalar.copy(gate_cols[:], gate_turned[:, 0, 0:E])
+        nc.scalar.copy(gate_cols[:], gate_turned[:, 0:E])
 
         w1t_s_dealt = tile("w1t_s_dealt", [P, K], U8, "dy_s")
         nc.vector.tensor_copy(
             w1t_s_dealt[:].rearrange("p (t m) -> p t m", t=PACK), w1t_s[:].rearrange("p (m t) -> p t m", t=PACK)
         )
 
-        def deal(e):
-            dealt = tile(f"w1t_dealt{e}", [P, K], U32)
-            dst = dealt[:].rearrange("p (t c i) -> p c t i", t=PACK, i=4)
-            src = w["w1t", e].rearrange("p (c i t) -> p c t i", t=PACK, i=4)
-            if "VSVV"[e] == "S":
-                nc.scalar.copy(dst, src)
-            else:
-                nc.vector.tensor_copy(
-                    dealt[:].bitcast(I32).rearrange("p (t c i) -> p c t i", t=PACK, i=4),
-                    w["w1t", e].bitcast(I32).rearrange("p (c i t) -> p c t i", t=PACK, i=4),
-                )
-            return dealt
-
         da_mx, dx = {}, {}
 
         def hidden(e):
-            dh = first_product("w2t", 4, gathered["dy", e], w2t_s, e)
+            dh = first_product("w2t", DH_BANK, gathered["dy", e], w2t_s, e)
             da = tile(f"da{e}", [P, H], BF16)
             nc.vector.scalar_tensor_tensor(da[:], dh[:], gate_cols[:, e : e + 1], slope[e][:], MULT, MULT)
-            pairs = da[:].bitcast(F32)
+            two_i = da[:].bitcast(F32)
             turned = bank_tile(f"turned{e}", [P, 2, P], e % 2)
             for u in range(2):
-                nc.tensor.transpose(turned[:, u, :], pairs[:, u : H // 2 : 2], ident[:])
+                nc.tensor.transpose(turned[:, u, :], two_i[:, u : H // 2 : 2], ident[:])
             grouped = tile(f"da_grouped{e}", [P, C * PACK], BF16)
-            nc.scalar.copy(grouped[:].bitcast(F32).rearrange("p (j u) -> p j u", u=2), turned[:].rearrange("p u j -> p j u"))
+            nc.scalar.copy(
+                grouped[:].bitcast(F32).rearrange("p (j u) -> p j u", u=2), turned[:].rearrange("p u j -> p j u")
+            )
             codes, scales = tile(f"da_w{e}", [P, C], U32), tile(f"da_s{e}", [P, C], U8)
             nc.vector.quantize_mx(codes[:].bitcast(FP8X4), scales[:], grouped[:])
             da_mx[e] = (codes, scales)
 
         def second_product(e):
-            dealt = deal(e)
+            dealt = tile(f"w1t_dealt{e}", [P, K], U32)
+            dst, src = dealt[:], weight["w1t", e]
+            on_vector = e != DEALT_ON_SCALAR
+            if on_vector:
+                dst, src = dst.bitcast(I32), src.bitcast(I32)
+            copy_on(
+                on_vector,
+                dst.rearrange("p (t c i) -> p c t i", t=PACK, i=LINE),
+                src.rearrange("p (c i t) -> p c t i", t=PACK, i=LINE),
+            )
             codes, scales = da_mx[e]
-            bank = bank_tile(f"dx_sum{e}", [P, PACK, C], 2 + e)
+            bank = bank_tile(f"dx_sum{e}", [P, PACK, C], DX_BANK + e)
             for t in range(PACK):
                 cols = slice(t * P, (t + 1) * P)
                 nc.tensor.matmul_mx(
-                    bank[:, t, :], lhsT=dealt[:, cols].bitcast(FP8X4), lhsT_scale=w1t_s_dealt[4 * e : P, cols],
+                    bank[:, t, :], lhsT=dealt[:, cols].bitcast(FP8X4),
+                    lhsT_scale=w1t_s_dealt[SCALE_ROWS * e : P, cols],
                     rhs=codes[:].bitcast(FP8X4), rhs_scale=scales[:], start=True, stop=True,
                 )
             dx[e] = tile(f"dx{e}", [P, PACK, C], F32)
-            if "VSSS"[e] == "S":
-                nc.scalar.copy(dx[e][:], bank[:])
-            else:
-                nc.vector.tensor_copy(dx[e][:], bank[:])
-
-        def scatter(e):
-            for t in (0, 2, 1, 3):
-                if ["VVSS","VVSS","VVSS","VVSS"][e][t] == "V":
-                    nc.vector.tensor_copy(windows[t][:].indirect(slots(e)), dx[e][:, t, :])
-                else:
-                    nc.scalar.activation(windows[t][:].indirect(slots(e)), dx[e][:, t, :], COPY)
+            copy_on(e == EMPTIED_ON_VECTOR, dx[e][:], bank[:])
 
         hidden(0)
-        hidden(1)
-        second_product(0)
-        hidden(2)
-        second_product(1)
-        hidden(3)
-        second_product(2)
-        second_product(3)
-        over = (None, None, None, None)
-        windows = [tile(f"window{t}", [P, T], F32, over[t]) for t in range(PACK)]
         for e in range(E):
-            scatter(e)
+            if e + 1 < E:
+                hidden(e + 1)
+            second_product(e)
+
+        windows = [tile(f"window{t}", [P, T], F32) for t in range(PACK)]
+        for e in range(E):
+            for j in range(VECTOR_WINDOWS):
+                nc.vector.tensor_copy(windows[j][:].indirect(entries(e, e + 1)), dx[e][:, j, :])
+                t = VECTOR_WINDOWS + j
+                nc.scalar.activation(windows[t][:].indirect(entries(e, e + 1)), dx[e][:, t, :], COPY)
 
         rows = out_0.rearrange("(p t) n -> t p n", t=PACK)
         rounded = tile("rounded", [P, PACK, T], BF16)
-        for t in (0, 2, 1, 3):
-            nc.sync.dma_start(rows[t], windows[t][:])
-            if "VVSV"[t] == "V":
-                nc.vector.tensor_copy(rounded[:, t, :], windows[t][:])
-            else:
-                nc.scalar.copy(rounded[:, t, :], windows[t][:])
+        for j in range(VECTOR_WINDOWS):
+            for t in (j, VECTOR_WINDOWS + j):
+                nc.sync.dma_start(rows[t], windows[t][:])
+                copy_on(t != ROUNDED_ON_SCALAR, rounded[:, t, :], windows[t][:])
 
         out_w, out_s = tile("out_w", [P, T], U32), tile("out_s", [P, T], U8)
         out_words = out_1[0].rearrange("p n d -> p (n d)").bitcast(I32)
         for h in range(2):
             cols = slice(h * HALF, (h + 1) * HALF)
             woven = tile(f"woven{h}", [P, HALF * PACK], BF16)
-            dst = woven[:].rearrange("p (c i t) -> p c t i", t=PACK, i=4)
-            src = rounded[:, :, cols].rearrange("p t (c i) -> p c t i", i=4)
-            if h == 0:
-                nc.vector.tensor_copy(dst, src)
-            else:
-                nc.scalar.copy(dst, src)
+            copy_on(
+                h == 0,
+                woven[:].rearrange("p (c i t) -> p c t i", t=PACK, i=LINE),
+                rounded[:, :, cols].rearrange("p t (c i) -> p c t i", i=LINE),
+            )
             nc.vector.quantize_mx(out_w[:, cols].bitcast(FP8X4), out_s[:, cols], woven[:])
             nc.sync.dma_start(out_words[:, cols], out_w[:, cols].bitcast(I32))
         for q in range(QUADS):
-            (nc.sync, nc.scalar)[q % 2].dma_start(out_2[0, 4 * q : 4 * q + 4, :].bitcast(I32), out_s[32 * q : 32 * q + 4, :].bitcast(I32))
+            queue = (nc.sync, nc.scalar)[q % 2]
+            queue.dma_start(
+                out_2[0, scale_rows(q), :].bitcast(I32), out_s[32 * q : 32 * q + SCALE_ROWS, :].bitcast(I32)
+            )

from contextlib import ExitStack

import concourse.mybir as mybir
from concourse.masks import make_identity

K, T, E, C, H, N = 512, 512, 4, 128, 512, 512
FLOPS = 2 * E * C * (K * H + N * H + H * K)

F32 = mybir.dt.float32
BF16 = mybir.dt.bfloat16
I32 = mybir.dt.int32
U32 = mybir.dt.uint32
U16 = mybir.dt.uint16
U8 = mybir.dt.uint8
FP8X4 = mybir.dt.float8_e4m3fn_x4
MULT = mybir.AluOpType.mult
RELU = mybir.ActivationFunctionType.Relu
COPY = mybir.ActivationFunctionType.Copy

P = 128
PACK = 4
QUADS = 4
LINE = 4
LIST_COLS = C // 16
SCALE_ROWS = 4
PAIR = 2
HALF = T // 2

VECTOR_WINDOWS = 2
DEALT_ON_SCALAR = 1
EMPTIED_ON_VECTOR = 0
ROUNDED_ON_SCALAR = VECTOR_WINDOWS

A_BANK, DH_BANK, DX_BANK = 0, E, 2


def tile_moe_rec_mlp_relu2_kernel(
    tc, x_words, x_scales, dy_words, dy_scales, w1_words, w1_scales, w2t_words, w2t_scales,
    w1t_words, w1t_scales, gate, offs, out_0, out_1, out_2,
):
    nc = tc.nc
    with ExitStack() as ctx:
        sb = ctx.enter_context(tc.tile_pool(name="sb", bufs=1))
        ps = ctx.enter_context(tc.psum_pool(name="ps", bufs=1))

        def tile(name, shape, dtype, over=None):
            return sb.tile(shape, dtype, name=name, tag=over or name, align_bytes=64)

        def bank_tile(name, shape, bank):
            return ps.tile(shape, F32, name=name, tag=f"bank{bank}")

        def copy_on(on_vector, dst, src):
            if on_vector:
                nc.vector.tensor_copy(dst, src)
            else:
                nc.scalar.copy(dst, src)

        offsets = sb.tile([P, E * LIST_COLS], U16, name="offsets")
        x_w, dy_w = tile("x_w", [P, T], U32), tile("dy_w", [P, T], U32)
        x_s, dy_s = tile("x_s", [P, T], U8), tile("dy_s", [P, T], U8)
        w1_s, w2t_s, w1t_s = tile("w1_s", [P, H], U8), tile("w2t_s", [P, H], U8), tile("w1t_s", [P, K], U8)
        gate_rows = tile("gate_rows", [P, C], F32)
        ident = tile("ident", [P, P], F32)

        nc.vector.memset(ident[:], 0.0)
        for plane in (w1t_s, x_s, w1_s, dy_s, w2t_s):
            nc.vector.memset(plane[:].bitcast(I32), 0)
        nc.vector.memset(gate_rows[:], 0.0)
        make_identity(nc, ident[:], nomemset=True)

        def load_token_words(dst, words):
            nc.sync.dma_start(dst[:].bitcast(I32), words[0].rearrange("p n d -> p (n d)").bitcast(I32))

        def scale_rows(q):
            return slice(SCALE_ROWS * q, SCALE_ROWS * (q + 1))

        def load_token_scales(dst, scales):
            for q in range(QUADS):
                nc.sync.dma_start(
                    dst[32 * q : 32 * q + SCALE_ROWS, :].bitcast(I32), scales[0, scale_rows(q), :].bitcast(I32)
                )

        def load_weight_scales(queue, dst, scales):
            for q in range(QUADS):
                queue.dma_start(
                    dst[32 * q : 32 * q + SCALE_ROWS * E, :].bitcast(I32), scales[:, 0, scale_rows(q), :].bitcast(I32)
                )

        weight = {}

        def load_weight(name, words, e0):
            dst = tile(f"{name}_{e0}", [P, PAIR, 512], U32)
            src = words[e0 : e0 + PAIR, 0].rearrange("e p n d -> p e (n d)")
            nc.sync.dma_start(dst[:].bitcast(I32), src.bitcast(I32))
            for j in range(PAIR):
                weight[name, e0 + j] = dst[:, j, :]

        def load_weight_and_scales(name, words, scales_queue, plane, scales):
            load_weight(name, words, 0)
            load_weight_scales(scales_queue, plane, scales)
            load_weight(name, words, PAIR)

        nc.sync.dma_start(offsets[:], offs)
        load_token_words(x_w, x_words)
        load_token_scales(x_s, x_scales)
        load_token_words(dy_w, dy_words)
        load_weight_and_scales("w1", w1_words, nc.sync, w1_s, w1_scales)
        load_token_scales(dy_s, dy_scales)
        nc.sync.dma_start(gate_rows[0:E, :], gate[0].rearrange("(e u) -> e u", e=E))
        load_weight_and_scales("w2t", w2t_words, nc.sync, w2t_s, w2t_scales)
        load_weight_and_scales("w1t", w1t_words, nc.gpsimd, w1t_s, w1t_scales)

        def entries(e0, e1):
            return offsets[:, e0 * LIST_COLS : e1 * LIST_COLS]

        gathered = {}

        def gather(name, words, scales, e0):
            g_w, g_s = tile(f"{name}_gw{e0}", [P, PAIR * C], U32), tile(f"{name}_gs{e0}", [P, PAIR * C], U8)
            nc.vector.tensor_copy(g_w[:], words[:].indirect(entries(e0, e0 + PAIR)))
            nc.vector.tensor_copy(g_s[:], scales[:].indirect(entries(e0, e0 + PAIR)))
            for j in range(PAIR):
                gathered[name, e0 + j] = (g_w[:, j * C : (j + 1) * C], g_s[:, j * C : (j + 1) * C])

        for e0 in range(0, E, PAIR):
            gather("x", x_w, x_s, e0)
            gather("dy", dy_w, dy_s, e0)

        def first_product(name, first_bank, tokens, plane, e):
            bank = bank_tile(f"{name}_sum{e}", [P, H], first_bank + e)
            nc.tensor.matmul_mx(
                bank[:], lhsT=tokens[0].bitcast(FP8X4), lhsT_scale=tokens[1],
                rhs=weight[name, e].bitcast(FP8X4), rhs_scale=plane[SCALE_ROWS * e : P, :], start=True, stop=True,
            )
            return bank

        slope = {}
        for e in range(E):
            a = first_product("w1", A_BANK, gathered["x", e], w1_s, e)
            slope[e] = tile(f"slope{e}", [P, H], F32)
            nc.scalar.activation(slope[e][:], a[:], RELU, scale=2.0)

        gate_turned = bank_tile("gate_turned", [P, P], DH_BANK)
        nc.tensor.transpose(gate_turned[:], gate_rows[:], ident[:])
        gate_cols = tile("gate_cols", [P, E], F32)
        nc.scalar.copy(gate_cols[:], gate_turned[:, 0:E])

        w1t_s_dealt = tile("w1t_s_dealt", [P, K], U8, "dy_s")
        nc.vector.tensor_copy(
            w1t_s_dealt[:].rearrange("p (t m) -> p t m", t=PACK), w1t_s[:].rearrange("p (m t) -> p t m", t=PACK)
        )

        da_mx, dx = {}, {}

        def hidden(e):
            dh = first_product("w2t", DH_BANK, gathered["dy", e], w2t_s, e)
            da = tile(f"da{e}", [P, H], BF16)
            nc.vector.scalar_tensor_tensor(da[:], dh[:], gate_cols[:, e : e + 1], slope[e][:], MULT, MULT)
            two_i = da[:].bitcast(F32)
            turned = bank_tile(f"turned{e}", [P, 2, P], e % 2)
            for u in range(2):
                nc.tensor.transpose(turned[:, u, :], two_i[:, u : H // 2 : 2], ident[:])
            grouped = tile(f"da_grouped{e}", [P, C * PACK], BF16)
            nc.scalar.copy(
                grouped[:].bitcast(F32).rearrange("p (j u) -> p j u", u=2), turned[:].rearrange("p u j -> p j u")
            )
            codes, scales = tile(f"da_w{e}", [P, C], U32), tile(f"da_s{e}", [P, C], U8)
            nc.vector.quantize_mx(codes[:].bitcast(FP8X4), scales[:], grouped[:])
            da_mx[e] = (codes, scales)

        def second_product(e):
            dealt = tile(f"w1t_dealt{e}", [P, K], U32)
            dst, src = dealt[:], weight["w1t", e]
            on_vector = e != DEALT_ON_SCALAR
            if on_vector:
                dst, src = dst.bitcast(I32), src.bitcast(I32)
            copy_on(
                on_vector,
                dst.rearrange("p (t c i) -> p c t i", t=PACK, i=LINE),
                src.rearrange("p (c i t) -> p c t i", t=PACK, i=LINE),
            )
            codes, scales = da_mx[e]
            bank = bank_tile(f"dx_sum{e}", [P, PACK, C], DX_BANK + e)
            for t in range(PACK):
                cols = slice(t * P, (t + 1) * P)
                nc.tensor.matmul_mx(
                    bank[:, t, :], lhsT=dealt[:, cols].bitcast(FP8X4),
                    lhsT_scale=w1t_s_dealt[SCALE_ROWS * e : P, cols],
                    rhs=codes[:].bitcast(FP8X4), rhs_scale=scales[:], start=True, stop=True,
                )
            dx[e] = tile(f"dx{e}", [P, PACK, C], F32)
            copy_on(e == EMPTIED_ON_VECTOR, dx[e][:], bank[:])

        hidden(0)
        for e in range(E):
            if e + 1 < E:
                hidden(e + 1)
            second_product(e)

        windows = [tile(f"window{t}", [P, T], F32) for t in range(PACK)]
        for e in range(E):
            for j in range(VECTOR_WINDOWS):
                nc.vector.tensor_copy(windows[j][:].indirect(entries(e, e + 1)), dx[e][:, j, :])
                t = VECTOR_WINDOWS + j
                nc.scalar.activation(windows[t][:].indirect(entries(e, e + 1)), dx[e][:, t, :], COPY)

        rows = out_0.rearrange("(p t) n -> t p n", t=PACK)
        rounded = tile("rounded", [P, PACK, T], BF16)
        for j in range(VECTOR_WINDOWS):
            for t in (j, VECTOR_WINDOWS + j):
                nc.sync.dma_start(rows[t], windows[t][:])
                copy_on(t != ROUNDED_ON_SCALAR, rounded[:, t, :], windows[t][:])

        out_w, out_s = tile("out_w", [P, T], U32), tile("out_s", [P, T], U8)
        out_words = out_1[0].rearrange("p n d -> p (n d)").bitcast(I32)
        for h in range(2):
            cols = slice(h * HALF, (h + 1) * HALF)
            woven = tile(f"woven{h}", [P, HALF * PACK], BF16)
            copy_on(
                h == 0,
                woven[:].rearrange("p (c i t) -> p c t i", t=PACK, i=LINE),
                rounded[:, :, cols].rearrange("p t (c i) -> p c t i", i=LINE),
            )
            nc.vector.quantize_mx(out_w[:, cols].bitcast(FP8X4), out_s[:, cols], woven[:])
            nc.sync.dma_start(out_words[:, cols], out_w[:, cols].bitcast(I32))
        for q in range(QUADS):
            queue = (nc.sync, nc.scalar)[q % 2]
            queue.dma_start(
                out_2[0, scale_rows(q), :].bitcast(I32), out_s[32 * q : 32 * q + SCALE_ROWS, :].bitcast(I32)
            )
